import numpy as np
import ml_dtypes


def mxq(x, axis, fmt="e4m3"):
    dtype, down = {"e4m3": (ml_dtypes.float8_e4m3fn, 7), "e5m2": (ml_dtypes.float8_e5m2, 14)}[fmt]
    v = np.moveaxis(np.asarray(x, np.float32).astype(ml_dtypes.bfloat16).astype(np.float64), axis, -1)
    blocks = v.reshape(v.shape[:-1] + (-1, 32))
    amax = np.abs(blocks).max(-1, keepdims=True)
    byte = np.maximum(np.where(amax > 0, np.frexp(amax)[1] - 1 + 127, 0) - down, 1)
    scale = np.exp2(byte - 127.0)
    codes = (blocks / scale).astype(np.float32).astype(dtype).astype(np.float64)
    return np.moveaxis((codes * scale).reshape(v.shape), -1, axis)


WIDE = False


def mx_kscale(k):
    if not WIDE:
        return np.ones(k)
    levels = np.array([10, -10, 5, -5, 0])
    if k % 512:
        return np.exp2(np.random.permutation(np.resize(levels, k // 32))).repeat(32)
    a = np.empty((k // 512, 16))
    for p in range(k // 512):
        a[p, :8] = np.random.permutation(np.resize(levels, 8))
        for g in range(8):
            far = levels[np.abs(levels - a[p, g]) >= 10]
            a[p, g + 8] = far[np.random.randint(len(far))]
    return np.exp2(a.ravel()).repeat(32)


def f64(x):
    return np.asarray(x).astype(np.float64)


def striped(idx):
    return np.tile(idx.reshape(-1, 16).T, (8, 1)).astype(np.uint16)


def unstriped(offs):
    return offs[:16].T.reshape(-1).astype(np.int64)


def striped8(idx):
    return np.concatenate([x.reshape(-1, 16).T for x in idx]).astype(np.uint16)


def runs(offs, k):
    lists = np.stack([offs[16 * r : 16 * r + 16].T.reshape(-1) for r in range(8)]).astype(np.int64)
    return lists[np.arange(k) % 512 // 64]


def pack_weight(w):
    k, n = w.shape
    w = f64(np.asarray(w, np.float32).astype(ml_dtypes.bfloat16)).reshape(k // 32, 32, n)
    amax = np.abs(w).max(1)
    byte = np.clip(np.where(amax > 0, np.frexp(amax)[1] - 1 + 127 - 7, 1), 1, 254)
    scaled = (w * np.exp2(127.0 - byte)[:, None, :]).reshape(k, n).astype(np.float32)
    words = np.ascontiguousarray(scaled.reshape(k // 512, 128, 4, n).transpose(0, 1, 3, 2)).astype(ml_dtypes.float8_e4m3fn).view(np.uint8)
    return words, np.ascontiguousarray(byte.astype(np.uint8).reshape(k // 512, 16, n))


def unpack_weight(words, scales):
    g, p, n, _ = words.shape
    vals = np.ascontiguousarray(words).view(ml_dtypes.float8_e4m3fn).astype(np.float64) * np.repeat(np.exp2(scales.astype(np.float64) - 127.0), 8, axis=1)[..., None]
    return vals.transpose(0, 1, 3, 2).reshape(g * 512, n)


K, T, S, V, G, H, C = 512, 2048, 1024, 512, 2048, 512, 512


def setup_inputs():
    n = np.random.standard_normal
    s = mx_kscale(K)[:, None]
    packed_xT = pack_weight(n((K, T)) * s)
    packed_dT = pack_weight(n((K, G)) / s)
    return {
        "x_words": packed_xT[0],
        "x_scales": packed_xT[1],
        "d_words": packed_dT[0],
        "d_scales": packed_dT[1],
        "gs": (np.random.uniform(0.5, 1.5, (K, 1)) / s).astype(np.float32),
        "offs": striped(np.random.permutation(T)[:S]),
        "k1": striped8(np.random.randint(0, G, (8, H))),
        "n1": striped8(np.stack([np.random.permutation(S) for _ in range(8)])),
        "cand": striped(np.random.permutation(T)[:C]),
        "n2": striped8(np.stack([np.random.permutation(V) for _ in range(8)])),
        "n3": striped8(np.stack([np.random.permutation(V) for _ in range(8)])),
    }


def reference(x_words, x_scales, d_words, d_scales, gs, offs, k1, n1, cand, n2, n3):
    x_cand = unpack_weight(x_words, x_scales)[:, unstriped(cand)]
    d_k1 = unpack_weight(d_words, d_scales)[np.arange(K)[:, None], runs(k1, K)]
    xq = unpack_weight(x_words, x_scales)[:, unstriped(offs)]
    h = 0.0625 * (d_k1.T @ xq)
    ln = h[np.arange(H)[:, None], runs(n1, H)]
    sq = (ln) ** 2
    ms = sq.reshape(H, V, 2).sum(axis=2)
    z = f64(gs) * np.sqrt(ms + 0.1)
    s = 0.0625 * ((x_cand.T @ mxq(z, 0, "e4m3")))
    return 0.75 * ((s - (s[np.arange(C)[:, None], runs(n2, C)])) * (s - (s[np.arange(C)[:, None], runs(n3, C)])))

@@ -1,0 +1,228 @@
+from contextlib import ExitStack
+
+import concourse.mybir as mybir
+
+K, T, S, V, G, H, C = 512, 2048, 1024, 512, 2048, 512, 512
+FLOPS = 2 * K * H * S + 2 * K * C * V
+
+F32 = mybir.dt.float32
+BF16 = mybir.dt.bfloat16
+I32 = mybir.dt.int32
+U32 = mybir.dt.uint32
+U16 = mybir.dt.uint16
+U8 = mybir.dt.uint8
+FP8X4 = mybir.dt.float8_e4m3fn_x4
+ACT = mybir.ActivationFunctionType
+ALU = mybir.AluOpType
+
+P = 128
+PACK = 4
+BANK = 512
+LIST_ROWS = 16
+PIECES = (256, 128, 128)
+
+
+def tile_picked_pqcprmsquad_none_p_kernel(
+    tc, x_words, x_scales, d_words, d_scales, gs, offs, k1, n1, cand, n2, n3, out
+):
+    nc = tc.nc
+    with ExitStack() as ctx:
+        keep = ctx.enter_context(tc.tile_pool(name="keep", bufs=1))
+        psum = ctx.enter_context(tc.psum_pool(name="psum", bufs=8))
+
+        def held(name, width, dtype):
+            return keep.tile([P, width], dtype, name=name, align_bytes=64)
+
+        def entries(lst, first, count):
+            return lst[:, first // LIST_ROWS : (first + count) // LIST_ROWS]
+
+        k1_t = held("k1_t", H // LIST_ROWS, U16)
+        offs_t = held("offs_t", S // LIST_ROWS, U16)
+        cand_t = held("cand_t", C // LIST_ROWS, U16)
+        n1_t = held("n1_t", S // LIST_ROWS, U16)
+        n2_t = held("n2_t", V // LIST_ROWS, U16)
+        n3_t = held("n3_t", V // LIST_ROWS, U16)
+        dw = held("dw", G, U32)
+        ds = held("ds", G, U8)
+        xw = held("xw", T, U32)
+        xs = held("xs", T, U8)
+        gs_t = held("gs_t", PACK, F32)
+
+        nc.sync.dma_start(k1_t[:], k1)
+        nc.sync.dma_start(
+            ds[:].bitcast(I32), d_scales[0].bitcast(I32).unsqueeze(1).to_broadcast([16, 8, G // 4])
+        )
+        nc.sync.dma_start(offs_t[:], offs)
+        for q in range(4):
+            nc.sync.dma_start(
+                xs[32 * q : 32 * (q + 1), :].bitcast(I32),
+                x_scales[0, 4 * q : 4 * q + 4, :].bitcast(I32).unsqueeze(0).to_broadcast([8, 4, T // 4]),
+            )
+        nc.sync.dma_start(dw[:].bitcast(I32), d_words[0].rearrange("p n t -> p (n t)").bitcast(I32))
+        nc.sync.dma_start(xw[:].bitcast(I32), x_words[0].rearrange("p n t -> p (n t)").bitcast(I32))
+        nc.sync.dma_start(cand_t[:], cand)
+        nc.sync.dma_start(n1_t[:], n1)
+        nc.sync.dma_start(gs_t[:], gs.rearrange("(p t) o -> p (t o)", t=PACK))
+        nc.sync.dma_start(n2_t[:], n2)
+        nc.sync.dma_start(n3_t[:], n3)
+
+        s_gain = held("s_gain", 1, F32)
+        three_quarters = held("three_quarters", 1, F32)
+        nc.gpsimd.memset(three_quarters[:], 0.75)
+        nc.scalar.activation(s_gain[:], three_quarters[:], ACT.Sqrt, scale=0.0625 * 0.0625)
+
+        s_win = [held(f"s_win{t}", 2 * V, F32) for t in range(PACK)]
+        for t in range(PACK):
+            nc.gpsimd.memset(s_win[t][:, V:], 0.0)
+
+        dk_s_listed = held("dk_s_listed", H, U8)
+        nc.vector.tensor_copy(dk_s_listed[:], ds[:].indirect(k1_t[:]))
+        dk_s = held("dk_s", H, U8)
+        nc.vector.tensor_copy(
+            dk_s[:].rearrange("p (t m) -> p t m", t=PACK), dk_s_listed[:].rearrange("p (m t) -> p t m", t=PACK)
+        )
+        for r in range(1, 4):
+            nc.sync.dma_start(dk_s[r:P:32, :].bitcast(I32), dk_s[8 * r : P : 32, :].bitcast(I32))
+
+        dk_w_listed = held("dk_w_listed", H, U32)
+        nc.vector.tensor_copy(dk_w_listed[:], dw[:].indirect(k1_t[:]))
+        dk_w = held("dk_w", H, U32)
+        nc.vector.tensor_copy(
+            dk_w[:].rearrange("p (t m) -> p t m", t=PACK), dk_w_listed[:].rearrange("p (m t) -> p t m", t=PACK)
+        )
+
+        sq = [held(f"sq{t}", S, F32) for t in range(PACK)]
+        halves = range(S // BANK)
+        xq_s = [held(f"xq_s{half}", BANK, U8) for half in halves]
+        xq_w = [held(f"xq_w{half}", BANK, U32) for half in halves]
+        for half in halves:
+            picked = entries(offs_t, half * BANK, BANK)
+            nc.vector.tensor_copy(xq_s[half][:], xs[:].indirect(picked))
+            nc.vector.tensor_copy(xq_w[half][:], xw[:].indirect(picked))
+        for t in range(PACK):
+            cols = slice(t * P, (t + 1) * P)
+            for half in halves:
+                acc = psum.tile([P, BANK], F32, name="acc")
+                nc.tensor.matmul_mx(
+                    out=acc[:],
+                    lhsT=dk_w[:, cols].bitcast(FP8X4),
+                    lhsT_scale=dk_s[:, cols],
+                    rhs=xq_w[half][:].bitcast(FP8X4),
+                    rhs_scale=xq_s[half][:],
+                    start=True,
+                    stop=True,
+                )
+                nc.scalar.activation(sq[t][:, half * BANK : (half + 1) * BANK], acc[:], ACT.Square, scale=0.0625)
+
+        xc_s_listed = held("xc_s_listed", C, U8)
+        xc_s = held("xc_s", C, U8)
+        nc.vector.tensor_copy(xc_s_listed[:], xs[:].indirect(cand_t[:]))
+        nc.vector.tensor_copy(
+            xc_s[:].bitcast(I32).rearrange("p (t h j) -> p t h j", t=PACK, j=2),
+            xc_s_listed[:].bitcast(I32).rearrange("p (h t j) -> p t h j", t=PACK, j=2),
+        )
+        xc_w = held("xc_w", C, U32)
+        nc.vector.tensor_copy(
+            xc_w[:].rearrange("p (t h j) -> p h t j", t=PACK, j=8), xw[:].indirect(cand_t[:])
+        )
+
+        def line_up(v0, n, tiles, ms, tag):
+            lined = keep.tile([P, len(tiles) * 2 * n], F32, name=f"lined_{v0}_{tiles[0]}", tag=tag, align_bytes=64)
+            for place, t in enumerate(tiles):
+                nc.vector.tensor_copy(
+                    lined[:, place * 2 * n : (place + 1) * 2 * n], sq[t][:].indirect(entries(n1_t, 2 * v0, 2 * n))
+                )
+            nc.vector.tensor_tensor(
+                ms[:, tiles[0] * n : (tiles[-1] + 1) * n], lined[:, 0::2], lined[:, 1::2], ALU.add
+            )
+
+        def weigh_on_scalar(v0, n, ms, z):
+            root = held(f"root{v0}", PACK * n, F32)
+            nc.scalar.activation(root[:], ms[:], ACT.Sqrt, bias=0.1)
+            z_planes = held(f"z_planes{v0}", PACK * n, BF16)
+            for t in range(PACK):
+                cols = slice(t * n, (t + 1) * n)
+                nc.scalar.activation(z_planes[:, cols], root[:, cols], ACT.Copy, scale=gs_t[:, t : t + 1])
+            nc.scalar.copy(
+                z[:].rearrange("p (c i t) -> p c t i", t=PACK, i=4),
+                z_planes[:].rearrange("p (t c i) -> p c t i", t=PACK, i=4),
+            )
+
+        def weigh_on_vector(v0, n, ms, z):
+            root = held(f"root{v0}", PACK * n, F32)
+            nc.scalar.activation(
+                root[:].rearrange("p (v t) -> p v t", t=PACK),
+                ms[:].rearrange("p (t v) -> p v t", t=PACK),
+                ACT.Sqrt,
+                bias=0.1,
+            )
+            nc.vector.tensor_tensor(
+                z[:].rearrange("p (v t) -> p v t", t=PACK),
+                root[:].rearrange("p (v t) -> p v t", t=PACK),
+                gs_t[:].unsqueeze(1).to_broadcast([P, n, PACK]),
+                ALU.mult,
+            )
+
+        def score(v0, n, z, into):
+            z_w = held(f"z_w{v0}", n, U32)
+            z_s = held(f"z_s{v0}", n, U8)
+            nc.vector.quantize_mx(out=z_w[:].bitcast(FP8X4), scales=z_s[:], in_=z[:])
+            for t in range(PACK):
+                cols = slice(t * P, (t + 1) * P)
+                nc.tensor.matmul_mx(
+                    out=into[t],
+                    lhsT=xc_w[:, cols].bitcast(FP8X4),
+                    lhsT_scale=xc_s[:, cols],
+                    rhs=z_w[:].bitcast(FP8X4),
+                    rhs_scale=z_s[:],
+                    start=True,
+                    stop=True,
+                )
+
+        def leave_bank(t, vs, bank):
+            nc.scalar.activation(s_win[t][:, vs], bank, ACT.Copy, scale=s_gain[:])
+            nc.scalar.activation(s_plain[t][:, vs], bank, ACT.Copy, scale=s_gain[:])
+
+        s_early = [psum.tile([P, BANK], F32, name="acc") for t in range(PACK)]
+        s_late = psum.tile([P, BANK], F32, name="acc")
+        s_plain = [held(f"s_plain{t}", V, F32) for t in range(PACK)]
+        n0, n1_, n2_ = PIECES
+        ms = [held(f"ms{piece}", PACK * n, F32) for piece, n in enumerate(PIECES)]
+        z0 = keep.tile([P, PACK * n0], BF16, name="z0", tag="z0", align_bytes=64)
+        z1 = held("z1", PACK * n1_, BF16)
+        z2 = held("z2", PACK * n2_, BF16)
+        early = n0 + n1_
+
+        line_up(0, n0, (0, 1, 2, 3), ms[0], "lined")
+        weigh_on_scalar(0, n0, ms[0], z0)
+        line_up(n0, n1_, (0, 1, 2, 3), ms[1], "lined")
+        weigh_on_scalar(n0, n1_, ms[1], z1)
+        line_up(early, n2_, (0, 1), ms[2], "lined")
+        score(0, n0, z0, [s_early[t][:, :n0] for t in range(PACK)])
+        line_up(early, n2_, (2, 3), ms[2], "z0")
+        score(n0, n1_, z1, [s_early[t][:, n0:early] for t in range(PACK)])
+        weigh_on_vector(early, n2_, ms[2], z2)
+        leave_bank(0, slice(0, early), s_early[0][:, :early])
+        score(early, n2_, z2, [s_late[:, t * n2_ : (t + 1) * n2_] for t in range(PACK)])
+        for t in range(PACK):
+            leave_bank(t, slice(early, V), s_late[:, t * n2_ : (t + 1) * n2_])
+            if t + 1 < PACK:
+                leave_bank(t + 1, slice(0, early), s_early[t + 1][:, :early])
+
+        out_rows = out.rearrange("(h t j) v -> t h j v", t=PACK, j=8)
+        for t in range(PACK):
+            parts = 2 if t == PACK - 1 else 1
+            n = V // parts
+            for part in range(parts):
+                vs = slice(part * n, (part + 1) * n)
+                d2 = held(f"d2_{t}_{part}", n, F32)
+                d3 = held(f"d3_{t}_{part}", n, F32)
+                res = held(f"res_{t}_{part}", n, F32)
+                nc.vector.tensor_tensor(
+                    d2[:], s_win[t][:].indirect(entries(n2_t, part * n, n)), s_plain[t][:, vs], ALU.subtract
+                )
+                nc.vector.tensor_tensor(
+                    d3[:], s_win[t][:].indirect(entries(n3_t, part * n, n)), s_plain[t][:, vs], ALU.subtract
+                )
+                nc.vector.tensor_tensor(res[:], d2[:], d3[:], ALU.mult)
+                nc.sync.dma_start(out_rows[t][:, :, vs], res[:])

@@ -49,7 +49,7 @@ def tile_picked_pqcprmsquad_none_p_kernel(
         gs_t = held("gs_t", PACK, F32)
 
         nc.sync.dma_start(k1_t[:], k1)
-        nc.sync.dma_start(
+        nc.scalar.dma_start(
             ds[:].bitcast(I32), d_scales[0].bitcast(I32).unsqueeze(1).to_broadcast([16, 8, G // 4])
         )
         nc.sync.dma_start(offs_t[:], offs)
@@ -62,7 +62,7 @@ def tile_picked_pqcprmsquad_none_p_kernel(
         nc.sync.dma_start(xw[:].bitcast(I32), x_words[0].rearrange("p n t -> p (n t)").bitcast(I32))
         nc.sync.dma_start(cand_t[:], cand)
         nc.sync.dma_start(n1_t[:], n1)
-        nc.sync.dma_start(gs_t[:], gs.rearrange("(p t) o -> p (t o)", t=PACK))
+        nc.gpsimd.dma_start(gs_t[:], gs.rearrange("(p t) o -> p (t o)", t=PACK))
         nc.sync.dma_start(n2_t[:], n2)
         nc.sync.dma_start(n3_t[:], n3)
 
@@ -71,9 +71,10 @@ def tile_picked_pqcprmsquad_none_p_kernel(
         nc.gpsimd.memset(three_quarters[:], 0.75)
         nc.scalar.activation(s_gain[:], three_quarters[:], ACT.Sqrt, scale=0.0625 * 0.0625)
 
-        s_win = [held(f"s_win{t}", 2 * V, F32) for t in range(PACK)]
-        for t in range(PACK):
+        s_win = [held(f"s_win{t}", 2 * V, F32) for t in range(PACK - 1)]
+        for t in range(PACK - 1):
             nc.gpsimd.memset(s_win[t][:, V:], 0.0)
+        s_win.append(held("s_win_last", V, F32))
 
         dk_s_listed = held("dk_s_listed", H, U8)
         nc.vector.tensor_copy(dk_s_listed[:], ds[:].indirect(k1_t[:]))
@@ -126,103 +127,102 @@ def tile_picked_pqcprmsquad_none_p_kernel(
             xc_w[:].rearrange("p (t h j) -> p h t j", t=PACK, j=8), xw[:].indirect(cand_t[:])
         )
 
-        def line_up(v0, n, tiles, ms, tag):
-            lined = keep.tile([P, len(tiles) * 2 * n], F32, name=f"lined_{v0}_{tiles[0]}", tag=tag, align_bytes=64)
-            for place, t in enumerate(tiles):
-                nc.vector.tensor_copy(
-                    lined[:, place * 2 * n : (place + 1) * 2 * n], sq[t][:].indirect(entries(n1_t, 2 * v0, 2 * n))
-                )
-            nc.vector.tensor_tensor(
-                ms[:, tiles[0] * n : (tiles[-1] + 1) * n], lined[:, 0::2], lined[:, 1::2], ALU.add
-            )
+        z = [held(f"z{piece}", PACK * n, BF16) for piece, n in enumerate(PIECES)]
+        starts = [sum(PIECES[:piece]) for piece in range(len(PIECES))]
 
-        def weigh_on_scalar(v0, n, ms, z):
-            root = held(f"root{v0}", PACK * n, F32)
+        def line_up(t, v0, n):
+            lined = held(f"lined_{t}_{v0}", 2 * n, F32)
+            nc.vector.tensor_copy(lined[:], sq[t][:].indirect(entries(n1_t, 2 * v0, 2 * n)))
+            return lined
+
+        def weigh(t, v0, n, lined, adder):
+            ms = held(f"ms_{t}_{v0}", n, F32)
+            root = held(f"root_{t}_{v0}", n, F32)
+            adder.tensor_tensor(ms[:], lined[:, 0::2], lined[:, 1::2], ALU.add)
             nc.scalar.activation(root[:], ms[:], ACT.Sqrt, bias=0.1)
-            z_planes = held(f"z_planes{v0}", PACK * n, BF16)
-            for t in range(PACK):
-                cols = slice(t * n, (t + 1) * n)
-                nc.scalar.activation(z_planes[:, cols], root[:, cols], ACT.Copy, scale=gs_t[:, t : t + 1])
-            nc.scalar.copy(
-                z[:].rearrange("p (c i t) -> p c t i", t=PACK, i=4),
-                z_planes[:].rearrange("p (t c i) -> p c t i", t=PACK, i=4),
+            for piece, first in enumerate(starts):
+                if v0 <= first < v0 + n:
+                    nc.scalar.activation(
+                        z[piece][:, t::PACK],
+                        root[:, first - v0 : first - v0 + PIECES[piece]],
+                        ACT.Copy,
+                        scale=gs_t[:, t : t + 1],
+                    )
+
+        z_w = held("z_w", V, U32)
+        z_s = held("z_s", V, U8)
+
+        def quantise(piece):
+            vs = slice(starts[piece], starts[piece] + PIECES[piece])
+            nc.vector.quantize_mx(out=z_w[:, vs].bitcast(FP8X4), scales=z_s[:, vs], in_=z[piece][:])
+
+        def score(t, vs, into):
+            cols = slice(t * P, (t + 1) * P)
+            nc.tensor.matmul_mx(
+                out=into,
+                lhsT=xc_w[:, cols].bitcast(FP8X4),
+                lhsT_scale=xc_s[:, cols],
+                rhs=z_w[:, vs].bitcast(FP8X4),
+                rhs_scale=z_s[:, vs],
+                start=True,
+                stop=True,
             )
 
-        def weigh_on_vector(v0, n, ms, z):
-            root = held(f"root{v0}", PACK * n, F32)
-            nc.scalar.activation(
-                root[:].rearrange("p (v t) -> p v t", t=PACK),
-                ms[:].rearrange("p (t v) -> p v t", t=PACK),
-                ACT.Sqrt,
-                bias=0.1,
-            )
-            nc.vector.tensor_tensor(
-                z[:].rearrange("p (v t) -> p v t", t=PACK),
-                root[:].rearrange("p (v t) -> p v t", t=PACK),
-                gs_t[:].unsqueeze(1).to_broadcast([P, n, PACK]),
-                ALU.mult,
-            )
+        def leave_bank(into, bank):
+            nc.scalar.activation(into, bank, ACT.Copy, scale=s_gain[:])
 
-        def score(v0, n, z, into):
-            z_w = held(f"z_w{v0}", n, U32)
-            z_s = held(f"z_s{v0}", n, U8)
-            nc.vector.quantize_mx(out=z_w[:].bitcast(FP8X4), scales=z_s[:], in_=z[:])
-            for t in range(PACK):
-                cols = slice(t * P, (t + 1) * P)
-                nc.tensor.matmul_mx(
-                    out=into[t],
-                    lhsT=xc_w[:, cols].bitcast(FP8X4),
-                    lhsT_scale=xc_s[:, cols],
-                    rhs=z_w[:].bitcast(FP8X4),
-                    rhs_scale=z_s[:],
-                    start=True,
-                    stop=True,
-                )
+        for t in range(PACK - 1):
+            lined = [line_up(t, v0, V // 2) for v0 in (0, V // 2)]
+            for half in range(2):
+                weigh(t, half * V // 2, V // 2, lined[half], nc.gpsimd)
+        t = PACK - 1
+        lined = []
+        for piece, n in enumerate(PIECES):
+            lined.append(line_up(t, starts[piece], n))
+            if piece > 0:
+                weigh(t, starts[piece - 1], PIECES[piece - 1], lined[piece - 1], nc.vector)
+        weigh(t, starts[-1], PIECES[-1], lined[-1], nc.vector)
 
-        def leave_bank(t, vs, bank):
-            nc.scalar.activation(s_win[t][:, vs], bank, ACT.Copy, scale=s_gain[:])
-            nc.scalar.activation(s_plain[t][:, vs], bank, ACT.Copy, scale=s_gain[:])
-
-        s_early = [psum.tile([P, BANK], F32, name="acc") for t in range(PACK)]
+        s_bank = [psum.tile([P, BANK], F32, name="acc") for t in range(PACK)]
         s_late = psum.tile([P, BANK], F32, name="acc")
         s_plain = [held(f"s_plain{t}", V, F32) for t in range(PACK)]
-        n0, n1_, n2_ = PIECES
-        ms = [held(f"ms{piece}", PACK * n, F32) for piece, n in enumerate(PIECES)]
-        z0 = keep.tile([P, PACK * n0], BF16, name="z0", tag="z0", align_bytes=64)
-        z1 = held("z1", PACK * n1_, BF16)
-        z2 = held("z2", PACK * n2_, BF16)
-        early = n0 + n1_
-
-        line_up(0, n0, (0, 1, 2, 3), ms[0], "lined")
-        weigh_on_scalar(0, n0, ms[0], z0)
-        line_up(n0, n1_, (0, 1, 2, 3), ms[1], "lined")
-        weigh_on_scalar(n0, n1_, ms[1], z1)
-        line_up(early, n2_, (0, 1), ms[2], "lined")
-        score(0, n0, z0, [s_early[t][:, :n0] for t in range(PACK)])
-        line_up(early, n2_, (2, 3), ms[2], "z0")
-        score(n0, n1_, z1, [s_early[t][:, n0:early] for t in range(PACK)])
-        weigh_on_vector(early, n2_, ms[2], z2)
-        leave_bank(0, slice(0, early), s_early[0][:, :early])
-        score(early, n2_, z2, [s_late[:, t * n2_ : (t + 1) * n2_] for t in range(PACK)])
-        for t in range(PACK):
-            leave_bank(t, slice(early, V), s_late[:, t * n2_ : (t + 1) * n2_])
-            if t + 1 < PACK:
-                leave_bank(t + 1, slice(0, early), s_early[t + 1][:, :early])
+        late = starts[-1]
+        for piece, n in enumerate(PIECES[:-1]):
+            vs = slice(starts[piece], starts[piece] + n)
+            quantise(piece)
+            score(0, vs, s_bank[0][:, vs])
+        leave_bank(s_win[0][:, :late], s_bank[0][:, :late])
+        leave_bank(s_plain[0][:, :late], s_bank[0][:, :late])
+        quantise(len(PIECES) - 1)
+        score(0, slice(late, V), s_late[:, late:])
+        leave_bank(s_win[0][:, late:V], s_late[:, late:])
+        leave_bank(s_plain[0][:, late:], s_late[:, late:])
+        for t in range(1, PACK):
+            score(t, slice(0, V), s_bank[t][:])
+            leave_bank(s_win[t][:, :V], s_bank[t][:])
+            leave_bank(s_plain[t][:], s_bank[t][:])
 
         out_rows = out.rearrange("(h t j) v -> t h j v", t=PACK, j=8)
-        for t in range(PACK):
-            parts = 2 if t == PACK - 1 else 1
-            n = V // parts
-            for part in range(parts):
-                vs = slice(part * n, (part + 1) * n)
-                d2 = held(f"d2_{t}_{part}", n, F32)
-                d3 = held(f"d3_{t}_{part}", n, F32)
-                res = held(f"res_{t}_{part}", n, F32)
-                nc.vector.tensor_tensor(
-                    d2[:], s_win[t][:].indirect(entries(n2_t, part * n, n)), s_plain[t][:, vs], ALU.subtract
-                )
-                nc.vector.tensor_tensor(
-                    d3[:], s_win[t][:].indirect(entries(n3_t, part * n, n)), s_plain[t][:, vs], ALU.subtract
-                )
-                nc.vector.tensor_tensor(res[:], d2[:], d3[:], ALU.mult)
-                nc.sync.dma_start(out_rows[t][:, :, vs], res[:])
+
+        def difference(name, lst, t, v0, n):
+            diff = held(f"{name}_{t}_{v0}", n, F32)
+            nc.vector.tensor_tensor(
+                diff[:], s_win[t][:].indirect(entries(lst, v0, n)), s_plain[t][:, v0 : v0 + n], ALU.subtract
+            )
+            return diff
+
+        def finish(t, v0, n, d2, d3):
+            res = held(f"res_{t}_{v0}", n, F32)
+            nc.vector.tensor_tensor(res[:], d2[:], d3[:], ALU.mult)
+            nc.sync.dma_start(out_rows[t][:, :, v0 : v0 + n], res[:])
+
+        steps = [(t, 0, V) for t in range(PACK - 1)]
+        steps += [(PACK - 1, starts[piece], n) for piece, n in enumerate(PIECES)]
+        waiting = None
+        for t, v0, n in steps:
+            d2 = difference("d2", n2_t, t, v0, n)
+            if waiting is not None:
+                finish(*waiting)
+            d3 = difference("d3", n3_t, t, v0, n)
+            waiting = (t, v0, n, d2, d3)
+        finish(*waiting)

@@ -20,6 +20,7 @@ PACK = 4
 BANK = 512
 LIST_ROWS = 16
 PIECES = (256, 128, 128)
+STEP = 128
 
 
 def tile_picked_pqcprmsquad_none_p_kernel(
@@ -80,7 +81,8 @@ def tile_picked_pqcprmsquad_none_p_kernel(
         nc.vector.tensor_copy(dk_s_listed[:], ds[:].indirect(k1_t[:]))
         dk_s = held("dk_s", H, U8)
         nc.vector.tensor_copy(
-            dk_s[:].rearrange("p (t m) -> p t m", t=PACK), dk_s_listed[:].rearrange("p (m t) -> p t m", t=PACK)
+            dk_s[:].rearrange("p (t c i) -> p c t i", t=PACK, i=16),
+            dk_s_listed[:].rearrange("p (c i t) -> p c t i", t=PACK, i=16),
         )
         for r in range(1, 4):
             nc.sync.dma_start(dk_s[r:P:32, :].bitcast(I32), dk_s[8 * r : P : 32, :].bitcast(I32))
@@ -89,7 +91,8 @@ def tile_picked_pqcprmsquad_none_p_kernel(
         nc.vector.tensor_copy(dk_w_listed[:], dw[:].indirect(k1_t[:]))
         dk_w = held("dk_w", H, U32)
         nc.vector.tensor_copy(
-            dk_w[:].rearrange("p (t m) -> p t m", t=PACK), dk_w_listed[:].rearrange("p (m t) -> p t m", t=PACK)
+            dk_w[:].rearrange("p (t c i) -> p c t i", t=PACK, i=4),
+            dk_w_listed[:].rearrange("p (c i t) -> p c t i", t=PACK, i=4),
         )
 
         sq = [held(f"sq{t}", S, F32) for t in range(PACK)]
@@ -100,9 +103,9 @@ def tile_picked_pqcprmsquad_none_p_kernel(
             picked = entries(offs_t, half * BANK, BANK)
             nc.vector.tensor_copy(xq_s[half][:], xs[:].indirect(picked))
             nc.vector.tensor_copy(xq_w[half][:], xw[:].indirect(picked))
-        for t in range(PACK):
+        for t, half in [(0, 0), (1, 0), (0, 1), (1, 1), (2, 0), (2, 1), (3, 0), (3, 1)]:
             cols = slice(t * P, (t + 1) * P)
-            for half in halves:
+            if True:
                 acc = psum.tile([P, BANK], F32, name="acc")
                 nc.tensor.matmul_mx(
                     out=acc[:],
@@ -127,7 +130,7 @@ def tile_picked_pqcprmsquad_none_p_kernel(
             xc_w[:].rearrange("p (t h j) -> p h t j", t=PACK, j=8), xw[:].indirect(cand_t[:])
         )
 
-        z = [held(f"z{piece}", PACK * n, BF16) for piece, n in enumerate(PIECES)]
+        z = held("z", PACK * V, BF16)
         starts = [sum(PIECES[:piece]) for piece in range(len(PIECES))]
 
         def line_up(t, v0, n):
@@ -140,21 +143,18 @@ def tile_picked_pqcprmsquad_none_p_kernel(
             root = held(f"root_{t}_{v0}", n, F32)
             adder.tensor_tensor(ms[:], lined[:, 0::2], lined[:, 1::2], ALU.add)
             nc.scalar.activation(root[:], ms[:], ACT.Sqrt, bias=0.1)
-            for piece, first in enumerate(starts):
-                if v0 <= first < v0 + n:
-                    nc.scalar.activation(
-                        z[piece][:, t::PACK],
-                        root[:, first - v0 : first - v0 + PIECES[piece]],
-                        ACT.Copy,
-                        scale=gs_t[:, t : t + 1],
-                    )
+            plane = z[:, PACK * v0 + t : PACK * (v0 + n) : PACK]
+            if t == PACK - 1 and v0 >= V // 2:
+                nc.vector.tensor_scalar(plane, root[:], gs_t[:, t : t + 1], None, ALU.mult)
+            else:
+                nc.scalar.activation(plane, root[:], ACT.Copy, scale=gs_t[:, t : t + 1])
 
         z_w = held("z_w", V, U32)
         z_s = held("z_s", V, U8)
 
         def quantise(piece):
             vs = slice(starts[piece], starts[piece] + PIECES[piece])
-            nc.vector.quantize_mx(out=z_w[:, vs].bitcast(FP8X4), scales=z_s[:, vs], in_=z[piece][:])
+            nc.vector.quantize_mx(out=z_w[:, vs].bitcast(FP8X4), scales=z_s[:, vs], in_=z[:, PACK * vs.start : PACK * vs.stop])
 
         def score(t, vs, into):
             cols = slice(t * P, (t + 1) * P)
@@ -171,32 +171,31 @@ def tile_picked_pqcprmsquad_none_p_kernel(
         def leave_bank(into, bank):
             nc.scalar.activation(into, bank, ACT.Copy, scale=s_gain[:])
 
-        for t in range(PACK - 1):
-            lined = [line_up(t, v0, V // 2) for v0 in (0, V // 2)]
-            for half in range(2):
-                weigh(t, half * V // 2, V // 2, lined[half], nc.gpsimd)
+        for t, widths in enumerate(((128, 128, 256), (256, 256), (256, 256))):
+            firsts = [sum(widths[:place]) for place in range(len(widths))]
+            lined = [line_up(t, v0, n) for v0, n in zip(firsts, widths)]
+            for place, n in enumerate(widths):
+                weigh(t, firsts[place], n, lined[place], nc.gpsimd)
         t = PACK - 1
-        lined = []
-        for piece, n in enumerate(PIECES):
-            lined.append(line_up(t, starts[piece], n))
-            if piece > 0:
-                weigh(t, starts[piece - 1], PIECES[piece - 1], lined[piece - 1], nc.vector)
-        weigh(t, starts[-1], PIECES[-1], lined[-1], nc.vector)
+        lined = [line_up(t, v0, STEP) for v0 in range(0, V, STEP)]
+        for place, v0 in enumerate(range(0, V, STEP)):
+            weigh(t, v0, STEP, lined[place], nc.gpsimd if v0 < V // 2 else nc.vector)
 
-        s_bank = [psum.tile([P, BANK], F32, name="acc") for t in range(PACK)]
-        s_late = psum.tile([P, BANK], F32, name="acc")
+        first_banks = [psum.tile([P, BANK], F32, name="acc") for piece in PIECES]
+        s_bank = [None] + [psum.tile([P, BANK], F32, name="acc") for t in range(1, PACK)]
         s_plain = [held(f"s_plain{t}", V, F32) for t in range(PACK)]
-        late = starts[-1]
-        for piece, n in enumerate(PIECES[:-1]):
-            vs = slice(starts[piece], starts[piece] + n)
-            quantise(piece)
-            score(0, vs, s_bank[0][:, vs])
-        leave_bank(s_win[0][:, :late], s_bank[0][:, :late])
-        leave_bank(s_plain[0][:, :late], s_bank[0][:, :late])
-        quantise(len(PIECES) - 1)
-        score(0, slice(late, V), s_late[:, late:])
-        leave_bank(s_win[0][:, late:V], s_late[:, late:])
-        leave_bank(s_plain[0][:, late:], s_late[:, late:])
+        spans = [slice(starts[piece], starts[piece] + n) for piece, n in enumerate(PIECES)]
+        quantise(0)
+        score(0, spans[0], first_banks[0][:, spans[0]])
+        quantise(1)
+        score(0, spans[1], first_banks[1][:, spans[1]])
+        nc.vector.tensor_scalar(s_win[0][:, spans[0]], first_banks[0][:, spans[0]], s_gain[:], None, ALU.mult)
+        quantise(2)
+        score(0, spans[2], first_banks[2][:, spans[2]])
+        nc.vector.tensor_scalar(s_plain[0][:, spans[0]], first_banks[0][:, spans[0]], s_gain[:], None, ALU.mult)
+        for piece in (1, 2):
+            leave_bank(s_win[0][:, spans[piece]], first_banks[piece][:, spans[piece]])
+            leave_bank(s_plain[0][:, spans[piece]], first_banks[piece][:, spans[piece]])
         for t in range(1, PACK):
             score(t, slice(0, V), s_bank[t][:])
             leave_bank(s_win[t][:, :V], s_bank[t][:])

from contextlib import ExitStack

import concourse.mybir as mybir

K, T, S, V, G, H, C = 512, 2048, 1024, 512, 2048, 512, 512
FLOPS = 2 * K * H * S + 2 * K * C * V

F32 = mybir.dt.float32
BF16 = mybir.dt.bfloat16
I32 = mybir.dt.int32
U32 = mybir.dt.uint32
U16 = mybir.dt.uint16
U8 = mybir.dt.uint8
FP8X4 = mybir.dt.float8_e4m3fn_x4
ACT = mybir.ActivationFunctionType
ALU = mybir.AluOpType

P = 128
PACK = 4
BANK = 512
LIST_ROWS = 16
PIECES = (256, 128, 128)
STEP = 128


def tile_picked_pqcprmsquad_none_p_kernel(
    tc, x_words, x_scales, d_words, d_scales, gs, offs, k1, n1, cand, n2, n3, out
):
    nc = tc.nc
    with ExitStack() as ctx:
        keep = ctx.enter_context(tc.tile_pool(name="keep", bufs=1))
        psum = ctx.enter_context(tc.psum_pool(name="psum", bufs=8))

        def held(name, width, dtype):
            return keep.tile([P, width], dtype, name=name, align_bytes=64)

        def entries(lst, first, count):
            return lst[:, first // LIST_ROWS : (first + count) // LIST_ROWS]

        k1_t = held("k1_t", H // LIST_ROWS, U16)
        offs_t = held("offs_t", S // LIST_ROWS, U16)
        cand_t = held("cand_t", C // LIST_ROWS, U16)
        n1_t = held("n1_t", S // LIST_ROWS, U16)
        n2_t = held("n2_t", V // LIST_ROWS, U16)
        n3_t = held("n3_t", V // LIST_ROWS, U16)
        dw = held("dw", G, U32)
        ds = held("ds", G, U8)
        xw = held("xw", T, U32)
        xs = held("xs", T, U8)
        gs_t = held("gs_t", PACK, F32)

        nc.sync.dma_start(k1_t[:], k1)
        nc.scalar.dma_start(
            ds[:].bitcast(I32), d_scales[0].bitcast(I32).unsqueeze(1).to_broadcast([16, 8, G // 4])
        )
        nc.sync.dma_start(offs_t[:], offs)
        for q in range(4):
            nc.sync.dma_start(
                xs[32 * q : 32 * (q + 1), :].bitcast(I32),
                x_scales[0, 4 * q : 4 * q + 4, :].bitcast(I32).unsqueeze(0).to_broadcast([8, 4, T // 4]),
            )
        nc.sync.dma_start(dw[:].bitcast(I32), d_words[0].rearrange("p n t -> p (n t)").bitcast(I32))
        nc.sync.dma_start(xw[:].bitcast(I32), x_words[0].rearrange("p n t -> p (n t)").bitcast(I32))
        nc.sync.dma_start(cand_t[:], cand)
        nc.sync.dma_start(n1_t[:], n1)
        nc.gpsimd.dma_start(gs_t[:], gs.rearrange("(p t) o -> p (t o)", t=PACK))
        nc.sync.dma_start(n2_t[:], n2)
        nc.sync.dma_start(n3_t[:], n3)

        s_gain = held("s_gain", 1, F32)
        three_quarters = held("three_quarters", 1, F32)
        nc.gpsimd.memset(three_quarters[:], 0.75)
        nc.scalar.activation(s_gain[:], three_quarters[:], ACT.Sqrt, scale=0.0625 * 0.0625)

        s_win = [held(f"s_win{t}", 2 * V, F32) for t in range(PACK - 1)]
        for t in range(PACK - 1):
            nc.gpsimd.memset(s_win[t][:, V:], 0.0)
        s_win.append(held("s_win_last", V, F32))

        dk_s_listed = held("dk_s_listed", H, U8)
        nc.vector.tensor_copy(dk_s_listed[:], ds[:].indirect(k1_t[:]))
        dk_s = held("dk_s", H, U8)
        nc.vector.tensor_copy(
            dk_s[:].rearrange("p (t c i) -> p c t i", t=PACK, i=16),
            dk_s_listed[:].rearrange("p (c i t) -> p c t i", t=PACK, i=16),
        )
        for r in range(1, 4):
            nc.sync.dma_start(dk_s[r:P:32, :].bitcast(I32), dk_s[8 * r : P : 32, :].bitcast(I32))

        dk_w_listed = held("dk_w_listed", H, U32)
        nc.vector.tensor_copy(dk_w_listed[:], dw[:].indirect(k1_t[:]))
        dk_w = held("dk_w", H, U32)
        nc.vector.tensor_copy(
            dk_w[:].rearrange("p (t c i) -> p c t i", t=PACK, i=4),
            dk_w_listed[:].rearrange("p (c i t) -> p c t i", t=PACK, i=4),
        )

        sq = [held(f"sq{t}", S, F32) for t in range(PACK)]
        halves = range(S // BANK)
        xq_s = [held(f"xq_s{half}", BANK, U8) for half in halves]
        xq_w = [held(f"xq_w{half}", BANK, U32) for half in halves]
        for half in halves:
            picked = entries(offs_t, half * BANK, BANK)
            nc.vector.tensor_copy(xq_s[half][:], xs[:].indirect(picked))
            nc.vector.tensor_copy(xq_w[half][:], xw[:].indirect(picked))
        for t, half in [(0, 0), (1, 0), (0, 1), (1, 1), (2, 0), (2, 1), (3, 0), (3, 1)]:
            cols = slice(t * P, (t + 1) * P)
            if True:
                acc = psum.tile([P, BANK], F32, name="acc")
                nc.tensor.matmul_mx(
                    out=acc[:],
                    lhsT=dk_w[:, cols].bitcast(FP8X4),
                    lhsT_scale=dk_s[:, cols],
                    rhs=xq_w[half][:].bitcast(FP8X4),
                    rhs_scale=xq_s[half][:],
                    start=True,
                    stop=True,
                )
                nc.scalar.activation(sq[t][:, half * BANK : (half + 1) * BANK], acc[:], ACT.Square, scale=0.0625)

        xc_s_listed = held("xc_s_listed", C, U8)
        xc_s = held("xc_s", C, U8)
        nc.vector.tensor_copy(xc_s_listed[:], xs[:].indirect(cand_t[:]))
        nc.vector.tensor_copy(
            xc_s[:].bitcast(I32).rearrange("p (t h j) -> p t h j", t=PACK, j=2),
            xc_s_listed[:].bitcast(I32).rearrange("p (h t j) -> p t h j", t=PACK, j=2),
        )
        xc_w = held("xc_w", C, U32)
        nc.vector.tensor_copy(
            xc_w[:].rearrange("p (t h j) -> p h t j", t=PACK, j=8), xw[:].indirect(cand_t[:])
        )

        z = held("z", PACK * V, BF16)
        starts = [sum(PIECES[:piece]) for piece in range(len(PIECES))]

        def line_up(t, v0, n):
            lined = held(f"lined_{t}_{v0}", 2 * n, F32)
            nc.vector.tensor_copy(lined[:], sq[t][:].indirect(entries(n1_t, 2 * v0, 2 * n)))
            return lined

        def weigh(t, v0, n, lined, adder):
            ms = held(f"ms_{t}_{v0}", n, F32)
            root = held(f"root_{t}_{v0}", n, F32)
            adder.tensor_tensor(ms[:], lined[:, 0::2], lined[:, 1::2], ALU.add)
            nc.scalar.activation(root[:], ms[:], ACT.Sqrt, bias=0.1)
            plane = z[:, PACK * v0 + t : PACK * (v0 + n) : PACK]
            if t == PACK - 1 and v0 >= V // 2:
                nc.vector.tensor_scalar(plane, root[:], gs_t[:, t : t + 1], None, ALU.mult)
            else:
                nc.scalar.activation(plane, root[:], ACT.Copy, scale=gs_t[:, t : t + 1])

        z_w = held("z_w", V, U32)
        z_s = held("z_s", V, U8)

        def quantise(piece):
            vs = slice(starts[piece], starts[piece] + PIECES[piece])
            nc.vector.quantize_mx(out=z_w[:, vs].bitcast(FP8X4), scales=z_s[:, vs], in_=z[:, PACK * vs.start : PACK * vs.stop])

        def score(t, vs, into):
            cols = slice(t * P, (t + 1) * P)
            nc.tensor.matmul_mx(
                out=into,
                lhsT=xc_w[:, cols].bitcast(FP8X4),
                lhsT_scale=xc_s[:, cols],
                rhs=z_w[:, vs].bitcast(FP8X4),
                rhs_scale=z_s[:, vs],
                start=True,
                stop=True,
            )

        def leave_bank(into, bank):
            nc.scalar.activation(into, bank, ACT.Copy, scale=s_gain[:])

        for t, widths in enumerate(((128, 128, 256), (256, 256), (256, 256))):
            firsts = [sum(widths[:place]) for place in range(len(widths))]
            lined = [line_up(t, v0, n) for v0, n in zip(firsts, widths)]
            for place, n in enumerate(widths):
                weigh(t, firsts[place], n, lined[place], nc.gpsimd)
        t = PACK - 1
        lined = [line_up(t, v0, STEP) for v0 in range(0, V, STEP)]
        for place, v0 in enumerate(range(0, V, STEP)):
            weigh(t, v0, STEP, lined[place], nc.gpsimd if v0 < V // 2 else nc.vector)

        first_banks = [psum.tile([P, BANK], F32, name="acc") for piece in PIECES]
        s_bank = [None] + [psum.tile([P, BANK], F32, name="acc") for t in range(1, PACK)]
        s_plain = [held(f"s_plain{t}", V, F32) for t in range(PACK)]
        spans = [slice(starts[piece], starts[piece] + n) for piece, n in enumerate(PIECES)]
        quantise(0)
        score(0, spans[0], first_banks[0][:, spans[0]])
        quantise(1)
        score(0, spans[1], first_banks[1][:, spans[1]])
        nc.vector.tensor_scalar(s_win[0][:, spans[0]], first_banks[0][:, spans[0]], s_gain[:], None, ALU.mult)
        quantise(2)
        score(0, spans[2], first_banks[2][:, spans[2]])
        nc.vector.tensor_scalar(s_plain[0][:, spans[0]], first_banks[0][:, spans[0]], s_gain[:], None, ALU.mult)
        for piece in (1, 2):
            leave_bank(s_win[0][:, spans[piece]], first_banks[piece][:, spans[piece]])
            leave_bank(s_plain[0][:, spans[piece]], first_banks[piece][:, spans[piece]])
        for t in range(1, PACK):
            score(t, slice(0, V), s_bank[t][:])
            leave_bank(s_win[t][:, :V], s_bank[t][:])
            leave_bank(s_plain[t][:], s_bank[t][:])

        out_rows = out.rearrange("(h t j) v -> t h j v", t=PACK, j=8)

        def difference(name, lst, t, v0, n):
            diff = held(f"{name}_{t}_{v0}", n, F32)
            nc.vector.tensor_tensor(
                diff[:], s_win[t][:].indirect(entries(lst, v0, n)), s_plain[t][:, v0 : v0 + n], ALU.subtract
            )
            return diff

        def finish(t, v0, n, d2, d3):
            res = held(f"res_{t}_{v0}", n, F32)
            nc.vector.tensor_tensor(res[:], d2[:], d3[:], ALU.mult)
            nc.sync.dma_start(out_rows[t][:, :, v0 : v0 + n], res[:])

        steps = [(t, 0, V) for t in range(PACK - 1)]
        steps += [(PACK - 1, starts[piece], n) for piece, n in enumerate(PIECES)]
        waiting = None
        for t, v0, n in steps:
            d2 = difference("d2", n2_t, t, v0, n)
            if waiting is not None:
                finish(*waiting)
            d3 = difference("d3", n3_t, t, v0, n)
            waiting = (t, v0, n, d2, d3)
        finish(*waiting)
